import numpy as np, ml_dtypes
CORES = [40,64,80,88,96,104,120,144]
N = 8
import mx_ref
BF = ml_dtypes.bfloat16
def gentries(a):
    return np.ascontiguousarray(a.reshape(8, 16, -1).transpose(0, 2, 1)).reshape(8, -1)
def gtable(e):
    e = np.asarray(e); return np.ascontiguousarray(e.reshape(8, -1, 16).transpose(0, 2, 1)).reshape(128, -1).astype(np.int32)
def gcols(t, e):
    v = np.concatenate([t.reshape(8, 16, -1, 4), np.zeros((8, 16, 1, 4), BF)], axis=2)
    return np.ascontiguousarray(np.stack([v[g][:, e[g]] for g in range(8)])).reshape(128, -1)
def tile(rs):
    return np.stack(rs, axis=2).reshape(128, -1).astype(BF)
def pick(q, e):
    c = np.concatenate([q[0].reshape(128, -1, 4), np.zeros((128, 1, 4), np.uint8)], axis=1); s = np.concatenate([q[1], np.ones((16, 1), np.uint8)], axis=1)
    return (np.ascontiguousarray(c[:, e].reshape(128, -1)), np.ascontiguousarray(s[:, e]))
def join(*qs):
    return (np.concatenate([q[0] for q in qs], axis=1), np.concatenate([q[1] for q in qs], axis=1))
def put(q, e, v):
    c, s = q[0].reshape(128, -1, 4).copy(), q[1].copy(); c[:, e] = v[0].reshape(128, -1, 4); s[:, e] = v[1]
    return (c.reshape(128, -1), s)
def pk(c, s):
    return (np.ascontiguousarray(c), mx_ref.live(s))
def emit(q):
    return q[0], q[1]
def packed(v, rng):
    q = [mx_ref.quantize(np.ascontiguousarray(v[r])) for r in range(N)]
    return np.stack([a for a, b in q]), np.stack([mx_ref.plane(b, rng) for a, b in q])
def values_of_codes():
    e, c = np.zeros((128, 128, 4), np.float32), np.zeros((128, 2, 4), np.uint8)
    e[np.arange(128), np.arange(128), 0] = 1
    c[:127, :, 0] = np.arange(256).reshape(2, 128).T[:127]
    return mx_ref.matmul(mx_ref.quantize(e.reshape(128, 512).astype(BF)), (c.reshape(128, 8), np.full((16, 2), 127, np.uint8))).T.reshape(-1).astype(np.float64)
CODE_VALUE, SCALE_VALUE = values_of_codes(), 2.0 ** (np.arange(256) - 127.0)
def decode(q):
    return (CODE_VALUE[q[0]].reshape(16, 8, -1, 4) * SCALE_VALUE[q[1]][:, None, :, None] + 0.0).reshape(128, -1).astype(np.float32)
def f(rng, *shape):
    return mx_ref.flush((rng.standard_normal(shape, dtype=np.float32) * np.exp2(rng.integers(-2, 3, shape[:-1] + (1,)))).astype(BF))
def wide(rng, *shape, cols=0):
    v = rng.standard_normal(shape, dtype=np.float32) * np.exp2(rng.integers(-12, 13, shape)).astype(np.float32)
    if cols: v *= np.repeat(np.exp2(rng.integers(-cols, cols + 1, shape[:-2] + (1, shape[-1] // 4))) * (rng.random(shape[:-2] + (1, shape[-1] // 4)) > 0.0625), 4, axis=-1).astype(np.float32)
    return mx_ref.flush(v.astype(BF))
C = 352
STEP = [1, 2, 4]
def big(v):
    v = v.astype(np.float32)
    v[np.abs(v) < np.float32(2.0 ** -16)] = 0
    return v.astype(BF)
def numbers_of(rng):
    return {"x": big(f(rng, N, 128, 4 * C)), "u": np.array(f(rng, N, 128, 512)), "v": np.array(f(rng, N, 128, 512))}
def stored(k, t):
    return {"gl": np.stack([gtable(k[r]) for r in range(N)]), "ht": np.stack([gtable(t[r]) for r in range(N)])}
def lists(rng):
    e = np.tile(np.arange(C), (N, 8, 1))
    k = np.stack([rng.permuted(e, axis=2), rng.permuted(e, axis=2)], axis=3).reshape(N, 8, 2 * C)
    return stored(k, rng.integers(0, C, (N, 8, C)))
def layers(rng):
    return big(f(rng, N, 128, 2048)).reshape(N, 8, 16, 4, 8, 16, 4)
def weights(rng, w):
    c, p = packed(np.ascontiguousarray(w).reshape(N, 128, 2048), rng)
    return {"wc": c, "ws": p}
def setup_inputs(rng):
    return {**numbers_of(rng), **lists(rng), **weights(rng, layers(rng))}
def setup_inputs_ties(rng):
    d = numbers_of(rng)
    o = rng.permutation(N)
    k = rng.integers(-1, 2, (N, 8, C)).astype(np.float32)
    k[o[1]] = 1
    x = d["x"].reshape(N, 8, 16, C, 4)
    x[:, :, 0] = 0
    x[:, :, 0, :, 0] = k.astype(BF)
    c = np.ones(N, np.float32)
    c[o[0]] = 0
    c[o[2]] = -1
    u = d["u"].reshape(N, 128, 128, 4)
    u[:, :, ::16] = 0
    for h in range(0, 128, 16): u[:, h, h, 0] = c.astype(BF)
    w = layers(rng)
    w[:, :, :, :, :, :8] = 0
    return {"x": x.reshape(N, 128, 4 * C), "u": u.reshape(N, 128, 512), "v": d["v"], **lists(rng), **weights(rng, w)}
def setup_inputs_near(rng):
    d = numbers_of(rng)
    o = rng.permutation(N) % 2
    k = np.where(o == 0, 2.0 ** -30, 1.0).astype(np.float32)
    x = np.zeros((N, 8, 16, C, 4), np.float32)
    s = rng.integers(-1, 2, (N, 8, C)) * k[:, None, None]
    x[:, :, 0, :, 0] = 1.125 * s
    x[:, :, 1, :, 0] = -1.25 * s
    for r in range(N):
        for g in rng.permutation(8)[:4]: x[r, g, 0, rng.integers(C), 0] = 2.0 ** 30 * rng.choice([-1.0, 1.0])
    i = np.arange(N)
    e = ((i ^ (i >> 1) ^ (i >> 2))[:, None] + rng.permutation(8)) % 2
    a = (1 + (2 * rng.integers(0, 64, (N, 8, 8, C, 4)) + 1) * 2.0 ** -7) * np.exp2(12.0 - rng.integers(8, 15, (N, 8, 8, C, 4)))
    a[:, :, 0, :, 0] = -1.96875 * 2.0 ** 12
    a = np.where(e[:, :, None, None, None] == 0, -2.0 ** 26, a)
    x[:, :, 8:] = np.where(rng.random((N, 8, 1, C, 1)) < 0.5, a, 0.0)
    u = d["u"].reshape(N, 128, 128, 4)
    u[:, :, ::16] = 0
    for h in range(0, 128, 16):
        u[:, h, h, 0] = (1.125 * k).astype(BF)
        u[:, h + 1, h, 0] = k.astype(BF)
    w = layers(rng)
    w[:, :, :8] = 0
    w[:, :, :, :, :, :8] = 0
    return {"x": x.reshape(N, 128, 4 * C).astype(BF), "u": u.reshape(N, 128, 512), "v": d["v"], **lists(rng), **weights(rng, w)}
def setup_inputs_late(rng):
    d = numbers_of(rng)
    c = (rng.permutation(N) % 2 * 2.0 - 1.0).astype(np.float32).astype(BF)
    x = d["x"].reshape(N, 8, 16, C, 4)
    x[:, :, 0] = c[:, None, None, None]
    u = d["u"].reshape(N, 128, 128, 4)
    u[:, :, ::16] = 0
    for h in range(0, 128, 16): u[:, h, h, 0] = 1
    w = layers(rng)
    w[:, :, :, :, :, 0] = (w[:, :, :, :, :, 0].astype(np.float32) * 4).astype(BF)
    return {"x": x.reshape(N, 128, 4 * C), "u": u.reshape(N, 128, 512), "v": d["v"], **lists(rng), **weights(rng, w)}
def setup_inputs_ends(rng):
    d = numbers_of(rng)
    o, e = rng.permutation(N) % 4, rng.permutation(N) % 4
    s = rng.choice([-1.0, 1.0], (N, 128, C, 4))
    s[o == 0] = -1
    s[o == 1] = rng.choice([-1.0, 1.0], (N, 1, C, 1))[o == 1]
    x = s * (0.955 + 0.02 * rng.random((N, 128, C, 4))) * 2.0 ** 30
    x[:, :8] = 0
    x[:, 13] = -240 * 2.0 ** 22
    x[:, 14] = -249 * 2.0 ** 22
    x[:, 15] = 0
    x[o == 3] = 2.0 ** -30
    size = np.where(o == 3, 2.0 ** -30, 2.0 ** 30)
    a = np.stack([rng.permutation(8) % 2 * 2.0 - 1.0 for r in range(N)]) * size[:, None]
    u = d["u"].reshape(N, 128, 128, 4)
    u[:, :, ::16] = a.astype(np.float32).astype(BF)[:, None, :, None]
    v = rng.choice([-1.0, 1.0], (N, 128, 512)) * size[:, None, None]
    t = rng.integers(0, C, (N, 8, C))
    t[o == 0] = C - 1
    t[o == 1] = 0
    t[o == 2] = rng.integers(0, 2, (8, C)) * (C - 1)
    k = rng.integers(0, C, (N, 8, 2 * C))
    k[e == 0] = C - 1
    k[e == 1] = 0
    k[e == 1, 7] = C - 1
    k[e == 2] = np.arange(2 * C) % 2 * (C - 1)
    w = np.zeros((N, 128, 4, 128, 4), np.float32)
    i = np.arange(128)
    for b in range(4):
        w[:, i, b, i, b] = np.where(o == 3, 16.0, -0.25)[:, None]
        for r in range(N):
            if o[r] < 3:
                w[r, :8, b, :8, b] = 64 * np.eye(8)
                w[r, 13:16, b, 13:16, b] = [[0, 0, -64], [0, 0, 64], [0, 0, 0]]
    return {"x": x.astype(np.float32).reshape(N, 128, 4 * C).astype(BF), "u": u.reshape(N, 128, 512), "v": v.astype(np.float32).astype(BF), **stored(k, t), **weights(rng, w.astype(BF))}
def setup_inputs_spread(rng):
    d = setup_inputs(rng)
    d["x"] = big(wide(rng, N, 128, 4 * C, cols=6))
    return d
def check_inputs(d):
    b = []
    for k in ("x", "u", "v"):
        a = np.abs(d[k].astype(np.float32))
        if not (np.isfinite(a).all() and ((a == 0) | (a >= 2.0 ** -30) & (a <= 2.0 ** 30)).all()): b.append("a value of " + k)
    for k in ("gl", "ht"):
        if not ((d[k] >= 0) & (d[k] < C)).all(): b.append("an entry of " + k)
    none, least, most = [emit(mx_ref.quantize(np.full((128, 16), k, np.float32).astype(BF)))[1][0, 0] for k in (0.0, 2.0 ** -30, 2.0 ** 30)]
    for r in range(N):
        if ((d["wc"][r] == 0x7F) | (d["wc"][r] == 0xFF)).any(): b.append("wc: a code that is no number")
        s = mx_ref.live(d["ws"][r])
        if ((s != none) & ((s < least) | (s > most))).any(): b.append("ws: a scale out of range")
        if (((d["wc"][r].reshape(16, 8, 512, 4) & 0x7F) != 0) & (s == none)[:, None, :, None]).any(): b.append("wc: a code other than zero under the scale of zeros")
    return b
def reference(x, u, v, gl, ht, wc, ws):
    qu = [mx_ref.quantize(u[r]) for r in range(N)]
    lay = [pk(wc[r], ws[r]) for r in range(N)]
    guest, host = [gentries(gl[r]) for r in range(N)], [gentries(ht[r]) for r in range(N)]
    now = [x[r] for r in range(N)]
    y, pl = np.zeros((N, 128, C), np.float32), np.zeros((N, 8, C), np.float32)
    for step in STEP:
        q = [mx_ref.quantize(now[r]) for r in range(N)]
        bit = [(mx_ref.matmul(qu[r], q[r])[::16] > 0).astype(np.int64) for r in range(N)]
        made = []
        for r in range(N):
            p = r ^ step
            at, there = np.zeros((9, C), np.int64), np.zeros((8, C), np.int64)
            at[0] = np.arange(C)
            for g in range(8):
                there[g] = host[p][g][at[g]]
                at[g + 1] = guest[r][g][2 * at[g] + bit[p][g][there[g]]]
            far = gcols(decode(q[p]).astype(BF), there)
            z = mx_ref.quantize(np.maximum(gcols(now[r], at[:8]).astype(np.float32), far.astype(np.float32)).astype(BF))
            made.append(tile([mx_ref.matmul(pick(lay[r], np.arange(128 * b, 128 * b + 128)), z) * np.float32(0.015625) + now[r][:, b::4].astype(np.float32) for b in range(4)]))
            pl[r] = at[1:]
        now = made
    oc, osc = np.zeros((N, 128, 4 * C), np.uint8), np.zeros((N, 16, C), np.uint8)
    for r in range(N):
        q = mx_ref.quantize(now[r])
        y[r] = mx_ref.matmul(mx_ref.quantize(v[r]), q)
        oc[r], osc[r] = emit(q)
    return {"y": y, "pl": pl, "oc": oc, "osc": osc}

@@ -1,0 +1,359 @@
+from concourse.bass import DstId, RemoteDMATransfer, IndirectOffsetOnAxis
+from concourse.mybir import dt, AluOpType, ActivationFunctionType
+
+C = 352
+STEP = [1, 2, 4]
+L = C // 16
+SLOTS = 8
+F8 = "float8_e4m3fn_x4"
+
+SCRATCH = {
+    "ut": ("sbuf", [128, 512], "bfloat16"), "uq": ("sbuf", [128, 128], F8), "us": ("sbuf", [128, 128], "uint8"),
+    "uqp": ("sbuf", [128, 256], F8), "usp": ("sbuf", [128, 256], "uint8"),
+    "vt": ("sbuf", [128, 512], "bfloat16"), "vq": ("sbuf", [128, 128], F8), "vs": ("sbuf", [128, 128], "uint8"),
+    "wq": ("sbuf", [128, 512], F8), "wsc": ("sbuf", [128, 512], "uint8"),
+    "idn1": ("sbuf", [128, 128], "float32"), "idn": ("sbuf", [128, 128], "float32"),
+    "et": ("sbuf", [128, 2048], "bfloat16"), "eq": ("sbuf", [128, 512], F8), "es": ("sbuf", [128, 512], "uint8"),
+    "hti": ("sbuf", [128, 3 * L], "int32"), "hto": ("sbuf", [128, 2 * L], "uint16"), "htn": ("sbuf", [128, L], "uint16"),
+    "glx": ("dram", [64, 88 * SLOTS], "int32"), "eo": ("sbuf", [128, 88 * SLOTS], "int32"),
+    "pc": ("sbuf", [128, 1], "int32"), "pi": ("sbuf", [128, 8], "int32"), "ixt": ("sbuf", [128, 1], "int32"),
+    "pf": ("sbuf", [128, 4], "float32"), "bc": ("sbuf", [128, 1], "float32"), "ini": ("sbuf", [128, 1], "float32"),
+    "uoi": ("sbuf", [128, 16], "int32"), "uoj": ("sbuf", [128, 16], "int32"), "uou": ("sbuf", [128, 16], "uint16"),
+    "jm": ("sbuf", [128, C], "float32"), "ramp": ("sbuf", [128, C], "float32"), "jv": ("sbuf", [128, L * SLOTS], "float32"),
+    "jp": ("sbuf", [128, L * SLOTS], "float32"), "hlf": ("sbuf", [128, L * SLOTS], "float32"), "mh": ("sbuf", [128, L * SLOTS], "float32"),
+    "mc": ("sbuf", [128, L * SLOTS], "float32"), "ji": ("sbuf", [128, L * SLOTS], "float32"),
+    "mask": ("sbuf", [128, C], "bfloat16"), "keep": ("sbuf", [128, C], "bfloat16"),
+    "mask2": ("sbuf", [128, C], "float32"), "a0": ("sbuf", [128, C], "float32"),
+    "t1": ("sbuf", [128, 44 * SLOTS], "float32"), "t2": ("sbuf", [128, 44 * SLOTS], "float32"), "sel": ("sbuf", [128, 44 * SLOTS], "float32"),
+    "sm": ("sbuf", [128, L * SLOTS], "float32"), "df": ("sbuf", [128, L * SLOTS], "float32"),
+    "em": ("sbuf", [128, L * SLOTS], "float32"), "etab": ("sbuf", [128, L * SLOTS], "float32"), "dtab": ("sbuf", [128, L * SLOTS], "float32"),
+    "zb": ("sbuf", [128, 2 * L], "bfloat16"),
+    "sg": ("sbuf", [128, 2 * C], "bfloat16"), "gm": ("sbuf", [128, 2 * C], "bfloat16"), "sc": ("sbuf", [128, 2 * C], "bfloat16"),
+    "nt": ("sbuf", [128, L * SLOTS], "float32"), "nf": ("sbuf", [128, L * SLOTS], "float32"), "nu": ("sbuf", [128, L * SLOTS], "uint16"),
+    "ya": ("sbuf", [128, C], "float32"), "yb": ("sbuf", [128, C], "float32"), "plr": ("sbuf", [128, C], "float32"),
+    "mk2": ("sbuf", [128, C], "float32"), "sc2": ("sbuf", [128, C], "float32"), "vl": ("sbuf", [128, L], "uint16"),
+    "x64": ("sbuf", [128, 4 * C], "bfloat16"), "ds": ("sbuf", [128, 4 * C], "bfloat16"), "mm": ("sbuf", [128, 4 * C], "bfloat16"),
+    "tf": ("sbuf", [128, 4 * C], "float32"), "yt": ("sbuf", [128, C], "float32"),
+    "pd": ("psum", [128, 2048], "float32"), "pw": ("psum", [128, 2048], "float32"),
+    "hr": ("sbuf", [128, L], "uint16"), "lb": ("dram", [640, 2 * L], "bfloat16"),
+}
+for _k in range(4):
+    SCRATCH["xt%d" % _k] = ("sbuf", [128, 4 * C], "bfloat16")
+    SCRATCH["xq%d" % _k] = ("sbuf", [128, C], F8)
+    SCRATCH["xs%d" % _k] = ("sbuf", [128, C], "uint8")
+for _k in range(3):
+    SCRATCH["rc%d" % _k] = ("sbuf", [128, C], F8)
+    SCRATCH["rs%d" % _k] = ("sbuf", [128, C], "uint8")
+    SCRATCH["zt%d" % _k] = ("sbuf", [128, 4 * C], "bfloat16")
+    SCRATCH["zq%d" % _k] = ("sbuf", [128, C], F8)
+    SCRATCH["zs%d" % _k] = ("sbuf", [128, C], "uint8")
+    SCRATCH["bl%d" % _k] = ("sbuf", [128, 2 * L], "bfloat16")
+    SCRATCH["bb%d" % _k] = ("sbuf", [128, L * SLOTS], "bfloat16")
+    SCRATCH["hq%d" % _k] = ("sbuf", [128, L], "uint16")
+    SCRATCH["ca%d" % _k] = ("sbuf", [128, C // 2], F8)
+    SCRATCH["sa%d" % _k] = ("sbuf", [128, C], "uint8")
+
+SEMAPHORES = ["ve", "se", "pe", "gp", "dx", "du", "dh", "dg", "dw", "dv", "ig", "do", "sent", "rz", "rh"]
+for _k in range(3):
+    SEMAPHORES += ["c%d" % _k, "ba%d" % _k, "bz%d" % _k, "h%d" % _k, "rc%d" % _k, "rb%d" % _k]
+
+
+def share(topo, src, dst, i, n):
+    return topo.engines(src, dst)[i::n]
+
+
+def send(g, core, T, topo, parts, n):
+    ts, total = [], 0
+    for i, (dst, a, b, sem) in enumerate(parts):
+        e = share(topo, core, dst, i, n)
+        rid, pid = topo.addr(dst, core)
+        ts.append(RemoteDMATransfer(dst_ids=[DstId(rid=rid, pnc=pid)], dma_engine_mask=sum(1 << j for j in e), remote_sem=T.sem[sem], srcs=[a], dsts=[b]))
+        total += len(e)
+    g.remote_dma_fused(ts, local_sem=T.sem.sent)
+    return total
+
+
+def handers(topo, core, partner):
+    r = [c for c in topo.cores_of(core) if c != core and topo.may_write(c, partner)]
+    return [c for c in r if topo.die(c) == topo.die(core)], [c for c in r if topo.die(c) != topo.die(core)]
+
+
+def u8(v):
+    return v.bitcast(dt.uint8)
+
+
+def hand_on(g, core, T, topo, home, near, far):
+    rank = T.rank_of(home)
+    mates = [T.cores[rank ^ s] for s in STEP]
+    sent = 0
+    if core in (near[0], far[0]):
+        i = 0 if core == near[0] else 1
+        h = C // 2
+        for k in range(3):
+            land = T["ca%d" % k]
+            g.wait_ge(T.sem["rc%d" % k], len(share(topo, home, core, i, 2)))
+            sent += send(g, core, T, topo, [(mates[k], u8(land[:, :]), u8(T["rc%d" % k][:, i * h:(i + 1) * h]), "c%d" % k)], 1)
+    else:
+        i = 0 if core == near[1] else 1
+        if i:
+            g.wait_ge(T.sem.rh, len(share(topo, home, core, 0, 1)))
+            sent += send(g, core, T, topo, [(mates[k], T.hr[:, :], T["hq%d" % k][:, :], "h%d" % k) for k in range(3)], 4)
+        g.wait_ge(T.sem.rz, len(share(topo, home, core, i, 2)))
+        for k in range(3):
+            if not i:
+                g.wait_ge(T.sem["rc%d" % k], len(share(topo, home, core, 0, 1)))
+                sent += send(g, core, T, topo, [(mates[k], T["sa%d" % k][:, :], T["rs%d" % k][:, :], "c%d" % k)], 1)
+            if k < 2:
+                g.wait_ge(T.sem["rb%d" % k], len(share(topo, home, core, i, 2)))
+                base = 128 * (k + 1)
+            else:
+                g.wait_ge(T.sem["rb%d" % k], 2 * len(share(topo, home, core, 0, 4)))
+                base = 512
+            parts = []
+            for m in (2 * i, 2 * i + 1):
+                a = base - 32 * m
+                parts.append((mates[k], T.lb[a:a + 128, :], T["bb%d" % k][:, 2 * L * m:2 * L * (m + 1)], ("bz%d" if i else "ba%d") % k))
+            sent += send(g, core, T, topo, parts, 2)
+    g.wait_ge(T.sem.sent, sent)
+
+
+def rank_program(g, core, T, topo):
+    rank = T.rank_of(core)
+    if rank is None:
+        for home in T.cores:
+            if core in topo.cores_of(home):
+                near, far = handers(topo, home, T.cores[T.rank_of(home) ^ STEP[0]])
+                if core in near[:2] + far[:2]:
+                    hand_on(g, core, T, topo, home, near, far)
+        return
+    A, AF = AluOpType, ActivationFunctionType
+    mates = [T.cores[rank ^ s] for s in STEP]
+    near, far = handers(topo, core, mates[0])
+    queue = {"ve": g.vector, "se": g.scalar, "pe": g.tensor, "gp": g, "sy": g.sync}
+    count, seen, sent = {"ve": 0, "se": 0, "pe": 0, "gp": 0}, {}, [0]
+
+    def need(e, *toks):
+        for t in toks:
+            if isinstance(t, list):
+                need(e, *t)
+            elif t is not None and seen.get((e, t[0]), 0) < t[1]:
+                queue[e].wait_ge(T.sem[t[0]], t[1])
+                seen[(e, t[0])] = t[1]
+
+    def op(e, call, *deps):
+        need(e, *deps)
+        count[e] += 1
+        call().then_inc(T.sem[e], 1)
+        return (e, count[e])
+
+    v, s, p = g.vector, g.scalar, g.tensor
+
+    def ts(out, in0, s1, s2, o0, o1=None, deps=()):
+        if o1 is None:
+            return op("ve", lambda: v.tensor_scalar(out, in0, s1, None, o0), *deps)
+        return op("ve", lambda: v.tensor_scalar(out, in0, s1, s2, o0, o1), *deps)
+
+    def tt(out, a, b, o, *deps):
+        return op("ve", lambda: v.tensor_tensor(out, a, b, o), *deps)
+
+    def cp(out, a, *deps):
+        return op("ve", lambda: v.tensor_copy(out, a), *deps)
+
+    def ms(ap, c, *deps):
+        return op("ve", lambda: v.memset(ap, c), *deps)
+
+    def act(out, a, f, *deps, scale=1.0):
+        if scale == 1.0:
+            return op("se", lambda: s.activation(out, a, f), *deps)
+        return op("se", lambda: s.activation(out, a, f, scale=scale), *deps)
+
+    def mm(out, q, qs, x, xs, *deps):
+        return op("pe", lambda: p.matmul_mx(out, q, qs, x, xs, True, True), *deps)
+
+    def out_to(parts, n):
+        sent[0] += send(g, core, T, topo, parts, n)
+
+    g.sync.dma_start(T.xt0[:, :], T.x[:, :]).then_inc(T.sem.dx, 16)
+    g.sync.dma_start(T.ut[:, :], T.u[:, :]).then_inc(T.sem.du, 16)
+    nh = 0
+    g.scalar.dma_start(T.hti[:, 2 * L:3 * L], T.ht[:, :]).then_inc(T.sem.dh, 16)
+    for d in range(2):
+        w = 16 * (d + 1)
+        g.scalar.dma_start(T.hti[w:128, L * d:L * d + L], T.ht[0:128 - w, :]).then_inc(T.sem.dh, 16)
+        g.scalar.dma_start(T.hti[0:w, L * d:L * d + L], T.ht[128 - w:128, :]).then_inc(T.sem.dh, 16)
+    dh = ("dh", 80)
+    for d in range(SLOTS):
+        w = d + 1
+        c = slice(88 * d, 88 * d + 88)
+        if w < 8:
+            g.scalar.dma_start(T.glx[8 * w:64, c], T.gl[0:128 - 16 * w, :]).then_inc(T.sem.dg, 16)
+            nh += 16
+        g.scalar.dma_start(T.glx[0:8 * w, c], T.gl[128 - 16 * w:128, :]).then_inc(T.sem.dg, 16)
+        nh += 16
+    dg = ("dg", nh)
+
+    def iota(ap, pat, base, cm, f=False):
+        if f:
+            return op("gp", lambda: g.iota(ap, pat, base, cm, allow_small_or_imprecise_dtypes=True))
+        return op("gp", lambda: g.iota(ap, pat, base, cm))
+    k_hlf = ms(T.hlf[:, :], 0.5)
+    k_one = ms(T.idn1[:, :], 1.0)
+    k_zb = ms(T.zb[:, :], 0.0)
+    k_bc = ms(T.bc[:, :], -2.0 ** -110)
+    g_pc = iota(T.pc[:, :], [[1, 1]], 0, 1)
+    g_uo = iota(T.uoi[:, :], [[-16, 2], [16, 8]], 112, 0)
+    g_jm = iota(T.jm[:, :], [[0, L], [1, 16]], 0, 0, True)
+    g_rm = iota(T.ramp[:, :], [[1, C]], 0, 0, True)
+    g_jv = iota(T.jv[:, :], [[0, SLOTS], [16, L]], 0, 0, True)
+    g_mh = op("gp", lambda: g.affine_select(T.mh[:, :], T.hlf[:, :], [[-16, SLOTS], [0, L]], A.is_ge, 0.0, -16, 1), k_hlf)
+    g_id = op("gp", lambda: g.affine_select(T.idn[:, :], T.idn1[:, :], [[-1, 128]], A.is_equal, 0.0, 0, 1), k_one)
+    k_p15 = ts(T.pi[:, 0:1], T.pc[:, :], 15, None, A.bitwise_and, deps=(g_pc,))
+    k_h = ts(T.pi[:, 1:2], T.pc[:, :], 3, 1, A.logical_shift_right, A.bitwise_and)
+    k_i1 = ts(T.pi[:, 2:3], T.pc[:, :], 1, 120, A.logical_shift_right, A.bitwise_and)
+    k_i2 = ts(T.pi[:, 3:4], T.pc[:, :], 7, None, A.bitwise_and)
+    k_uo = ts(T.uoj[:, :], T.uoi[:, :], 127, None, A.bitwise_and, deps=(g_uo,))
+    k_pf = cp(T.pf[:, 0:2], T.pi[:, 0:2], k_p15, k_h)
+    k_ix = tt(T.ixt[:, :], T.pi[:, 2:3], T.pi[:, 3:4], A.add, k_i1, k_i2)
+    k_uu = cp(T.uou[:, :], T.uoj[:, :], k_uo)
+    k_nh = ts(T.pf[:, 2:3], T.pf[:, 1:2], -1.0, 1.0, A.mult, A.add, deps=(k_pf,))
+    k_mask = ts(T.mask[:, :], T.jm[:, :], T.pf[:, 0:1], None, A.is_equal, deps=(g_jm, k_pf))
+    k_keep = ts(T.keep[:, :], T.jm[:, :], T.pf[:, 0:1], None, A.not_equal)
+    k_htn = cp(T.htn[:, :], T.hti[:, 2 * L:3 * L], dh)
+    k_hto = cp(T.hto[:, :], T.hti[:, 0:2 * L])
+    k_u = op("ve", lambda: v.quantize_mx(T.uq[:, :], T.us[:, :], T.ut[:, :]), ("du", 16))
+    k_up = cp(T.uqp[:, :].bitcast(dt.uint32), T.uq[:, :].bitcast(dt.uint32).indirect(T.uou[:, :]), k_u, k_uu)
+    k_us = act(T.usp[:, :], T.us[:, :].indirect(T.uou[:, :]), AF.Copy, k_u, k_uu)
+
+    need("gp", k_htn, k_zb)
+    out_to([(far[1], T.htn[:, :], T.hr[:, :], "rh")], 1)
+    out_to([(near[1], T.zb[:, :], T.lb[0:128, :], "rz"), (far[1], T.zb[:, :], T.lb[0:128, :], "rz")], 2)
+
+    xtok, k_tab, k_eq, k_static, pdread = [("dx", 16)], None, None, None, []
+    pltok = None
+    h = C // 2
+    for k in range(3):
+        xt, xq, xs = T["xt%d" % k], T["xq%d" % k], T["xs%d" % k]
+        rc, rs, bl, bb, hq = T["rc%d" % k], T["rs%d" % k], T["bl%d" % k], T["bb%d" % k], T["hq%d" % k]
+        zt, zq, zs, xn = T["zt%d" % k], T["zq%d" % k], T["zs%d" % k], T["xt%d" % (k + 1)]
+        mate = mates[k]
+        back = handers(topo, mate, core)
+        q0 = op("ve", lambda: v.quantize_mx(xq[:, :], xs[:, :], xt[:, :]), xtok)
+        need("gp", q0)
+        out_to([(far[0], u8(xq[:, h:C]), u8(T["ca%d" % k][:, :]), "rc%d" % k)][:0] +
+               [(near[0], u8(xq[:, 0:h]), u8(T["ca%d" % k][:, :]), "rc%d" % k), (far[0], u8(xq[:, h:C]), u8(T["ca%d" % k][:, :]), "rc%d" % k)], 2)
+        out_to([(near[1], xs[:, :], T["sa%d" % k][:, :], "rc%d" % k)], 1)
+        if k == 0:
+            need("gp", k_ix, dg)
+            g.indirect_dma_start(T.eo[:, :], None, T.glx[:], IndirectOffsetOnAxis(ap=T.ixt[:, 0:1], axis=0), bounds_check=63).then_inc(T.sem.ig, 16)
+        sgn = []
+        for d in range(2):
+            m = mm(T.pd[:, 512 * d:512 * d + C], T.uqp[:, 128 * d:128 * d + 128], T.usp[:, 128 * d:128 * d + 128], xq[:, :], xs[:, :], q0, k_up, k_us, pdread)
+            need("se", m, k_bc)
+            sgn.append(op("se", lambda d=d: s.activation(T.sg[:, C * d:C * d + C], T.pd[:, 512 * d:512 * d + C], AF.Sign, bias=T.bc[:, 0:1])))
+        k64 = act(T.x64[:, :], xt[:, :], AF.Copy, xtok, scale=64.0)
+        gs = [tt(T.gm[:, C * d:C * d + C], T.sg[:, C * d:C * d + C].indirect(T.hto[:, L * d:L * d + L]), T.mask[:, :], A.mult, sgn[d], k_hto, k_mask) for d in range(2)]
+        sc = [op("ve", lambda d=d: v.tensor_tensor_scan(T.sc[:, C * d:C * d + C], T.keep[:, :], T.gm[:, C * d:C * d + C], 0.0, A.mult, A.add), gs[d], k_keep) for d in range(2)]
+        k_bl = cp(bl[:, :], T.sc[:, 15:2 * C:16], sc)
+        need("gp", k_bl)
+        if k < 2:
+            a = 128 * (k + 1)
+            out_to([(c, bl[:, :], T.lb[a:a + 128, :], "rb%d" % k) for c in (near[1], far[1])], 2)
+        else:
+            out_to([(c, bl[:, :], T.lb[a:a + 128, :], "rb%d" % k) for a in (384, 512) for c in (near[1], far[1])], 4)
+        if k == 0:
+            z = ms(T.et[:, :], 0.0)
+            ec = [cp(T.et[:, 512 * b + b:512 * b + 512:4], T.idn[:, :], z, g_id) for b in range(4)]
+            k_eq = op("ve", lambda: v.quantize_mx(T.eq[:, :], T.es[:, :], T.et[:, :]), ec)
+            m2 = cp(T.mask2[:, :], T.mask[:, :])
+            m2 = ms(T.mask2[0:16, :], 0.0, m2)
+            a0 = ts(T.a0[:, :], T.mask[:, :], -1000.0, None, A.mult)
+            a0 = ts(T.a0[0:16, :], T.jm[0:16, :], 0.0, 16.0, A.is_equal, A.mult, deps=(a0,))
+            a0 = ms(T.a0[0:16, 0:1], 0.0, a0)
+            i0 = ms(T.ini[:, :], 0.0)
+            i0 = cp(T.ini[0:16, :], T.pf[0:16, 0:1], i0)
+            k_static = [m2, a0, i0]
+            mh = ms(T.mh[0:16, :], 0.5, g_mh)
+            jp = ts(T.jp[:, :], T.jv[:, :], T.pf[:, 0:1], None, A.add, deps=(g_jv,))
+            mc = ts(T.mc[:, :], T.mh[:, :], -2.0, 1.0, A.mult, A.add, deps=(mh,))
+            ji = tt(T.ji[:, :], T.jp[:, :], T.mc[:, :], A.mult, jp, mc)
+            e1 = ts(T.t1[:, :], T.eo[:, 0:88 * SLOTS:2], T.pf[:, 2:3], None, A.mult, deps=(("ig", 16), k_nh))
+            e2 = ts(T.t2[:, :], T.eo[:, 1:88 * SLOTS:2], T.pf[:, 1:2], None, A.mult)
+            e3 = tt(T.sel[:, :], T.t1[:, :], T.t2[:, :], A.add, e1, e2)
+            for d in range(SLOTS):
+                ee, oo = T.sel[:, 44 * d:44 * d + L], T.sel[:, 44 * d + L:44 * d + 2 * L]
+                sm = tt(T.sm[:, L * d:L * d + L], ee, oo, A.add, e3)
+                df = tt(T.df[:, L * d:L * d + L], oo, ee, A.subtract)
+            em = tt(T.em[:, :], T.sm[:, :], T.mh[:, :], A.mult, sm)
+            dtb = tt(T.dtab[:, :], T.df[:, :], T.mh[:, :], A.mult, df)
+            etb = tt(T.etab[:, :], T.em[:, :], T.ji[:, :], A.add, em, ji)
+            k_tab = [dtb, etb]
+        call = ("c%d" % k, sum(len(share(topo, c, core, 0, 1)) for c in (back[0][0], back[1][0], back[0][1])))
+        if k == 0:
+            need("sy", call)
+            g.sync.dma_start(u8(T.wq[:, :]), T.wc[:, :]).then_inc(T.sem.dw, 16)
+            g.sync.dma_start(T.wsc[:, :], T.ws[:, :]).then_inc(T.sem.dw, 16)
+            g.sync.dma_start(T.vt[:, :], T.v[:, :]).then_inc(T.sem.dv, 16)
+        dc = []
+        for b in range(4):
+            m = mm(T.pd[:, 512 * b:512 * b + C], T.eq[:, 128 * b:128 * b + 128], T.es[:, 128 * b:128 * b + 128], rc[:, :], rs[:, :], call, k_eq, sgn)
+            dc.append(act(T.ds[:, C * b:C * b + C], T.pd[:, 512 * b:512 * b + C], AF.Copy, m))
+        pdread = dc
+
+        def larger(b):
+            return tt(T.mm[:, C * b:C * b + C], T.ds[:, C * b:C * b + C].indirect(hq[:, :]), xt[:, b:4 * C:4], A.max,
+                      dc[b], ("h%d" % k, len(share(topo, back[1][1], core, 0, 4))))
+
+        def lists(a, e, *deps):
+            n1 = tt(T.nt[:, a:e], bb[:, a:e], T.dtab[:, a:e], A.mult, k_tab, *deps)
+            n2 = tt(T.nf[:, a:e], T.nt[:, a:e], T.etab[:, a:e], A.add, n1)
+            return cp(T.nu[:, a:e], T.nf[:, a:e], n2)
+        ba = ("ba%d" % k, 2 * len(share(topo, back[0][1], core, 0, 2)))
+        bz = ("bz%d" % k, 2 * len(share(topo, back[1][1], core, 0, 2)))
+        lg = [larger(0), larger(1)]
+        n1 = lists(0, 2 * L, ba)
+        n2 = lists(2 * L, L * SLOTS, bz)
+        lg += [larger(2), larger(3)]
+        win, tok, ys = T.ramp, g_rm, [T.ya, T.yb]
+        for d in range(6):
+            o = ys[d % 2]
+            tok = act(o[:, :], win[:, :].indirect(T.nu[:, L * d:L * d + L]), AF.Copy, tok, n1 if d < 2 else n2)
+            win = o
+        c6 = tt(T.mk2[:, :], win[:, :].indirect(T.nu[:, 6 * L:7 * L]), T.mask2[:, :], A.mult, tok, k_static)
+        c7 = op("ve", lambda: v.tensor_tensor_scan(T.sc2[:, :], T.a0[:, :], T.mk2[:, :], T.ini[:, 0:1], A.add, A.max), c6)
+        k_vl = cp(T.vl[:, :], T.sc2[:, 15:C:16], c7)
+        zc = []
+        for b in range(4):
+            o, w = zt[:, b:4 * C:4], T.mm[:, C * b:C * b + C].indirect(T.vl[:, :])
+            zc.append(cp(o, w, k_vl, lg) if b < 2 else act(o, w, AF.Copy, k_vl, lg))
+        if k == 2:
+            o = ys[0]
+            t6 = act(o[:, :], win[:, :].indirect(T.nu[:, 6 * L:7 * L]), AF.Copy, tok)
+            pltok = act(T.plr[:, :], o[:, :].indirect(T.nu[:, 7 * L:8 * L]), AF.Copy, t6)
+        qz = op("ve", lambda: v.quantize_mx(zq[:, :], zs[:, :], zt[:, :]), zc)
+        xtok = []
+        for b in range(4):
+            m = mm(T.pw[:, 512 * b:512 * b + C], T.wq[:, 128 * b:128 * b + 128], T.wsc[:, 128 * b:128 * b + 128], zq[:, :], zs[:, :], qz, ("dw", 32))
+            ad = tt(T.tf[:, C * b:C * b + C], T.pw[:, 512 * b:512 * b + C], T.x64[:, b:4 * C:4], A.add, m, k64)
+            xtok.append(act(xn[:, b:4 * C:4], T.tf[:, C * b:C * b + C], AF.Copy, ad, scale=2.0 ** -6))
+        if k == 0:
+            k_v = op("ve", lambda: v.quantize_mx(T.vq[:, :], T.vs[:, :], T.vt[:, :]), ("dv", 16))
+
+    do = [0]
+
+    def store(out, a, *deps):
+        need("sy", *deps)
+        g.sync.dma_start(out, a).then_inc(T.sem.do, 16)
+        do[0] += 16
+    store(T.pl[0:7, :], T.plr[16:128:16, :], pltok)
+    store(T.pl[7:8, :], T.plr[0:1, :])
+    q3 = op("ve", lambda: v.quantize_mx(T.xq3[:, :], T.xs3[:, :], T.xt3[:, :]), xtok)
+    m = mm(T.pd[:, 0:C], T.vq[:, :], T.vs[:, :], T.xq3[:, :], T.xs3[:, :], q3, k_v, pdread)
+    yc = cp(T.yt[:, :], T.pd[:, 0:C], m)
+    store(T.oc[:, :], u8(T.xq3[:, :]), q3)
+    store(T.y[:, :], T.yt[:, :], yc)
+    for b in range(4):
+        store(T.osc[4 * b:4 * b + 4, :], T.xs3[32 * b:32 * b + 4, :])
+    g.sync.wait_ge(T.sem.do, do[0])
+    for e in ("ve", "se", "pe", "gp"):
+        need("gp", (e, count[e]))
+    g.wait_ge(T.sem.sent, sent[0])

@@ -1,9 +1,11 @@
-from concourse.bass import DstId, RemoteDMATransfer, IndirectOffsetOnAxis
+from concourse.bass import DstId, RemoteDMATransfer
 from concourse.mybir import dt, AluOpType, ActivationFunctionType
 
 C = 352
 STEP = [1, 2, 4]
 L = C // 16
+LA = 12
+PARTS = [(0, 16 * LA), (16 * LA, C)]
 SLOTS = 8
 F8 = "float8_e4m3fn_x4"
 
@@ -14,9 +16,10 @@ SCRATCH = {
     "wq": ("sbuf", [128, 512], F8), "wsc": ("sbuf", [128, 512], "uint8"),
     "idn1": ("sbuf", [128, 128], "float32"), "idn": ("sbuf", [128, 128], "float32"),
     "et": ("sbuf", [128, 2048], "bfloat16"), "eq": ("sbuf", [128, 512], F8), "es": ("sbuf", [128, 512], "uint8"),
-    "hti": ("sbuf", [128, 3 * L], "int32"), "hto": ("sbuf", [128, 2 * L], "uint16"), "htn": ("sbuf", [128, L], "uint16"),
-    "glx": ("dram", [64, 88 * SLOTS], "int32"), "eo": ("sbuf", [128, 88 * SLOTS], "int32"),
-    "pc": ("sbuf", [128, 1], "int32"), "pi": ("sbuf", [128, 8], "int32"), "ixt": ("sbuf", [128, 1], "int32"),
+    "hti": ("sbuf", [128, 2 * L], "int32"), "htj": ("sbuf", [128, L], "int32"),
+    "hto": ("sbuf", [128, 2 * L], "uint16"), "htn": ("sbuf", [128, L], "uint16"),
+    "glc": ("dram", [8, 2 * 88 * SLOTS], "int32"), "eo": ("sbuf", [128, 88 * SLOTS], "int32"),
+    "pc": ("sbuf", [128, 1], "int32"), "pi": ("sbuf", [128, 8], "int32"),
     "pf": ("sbuf", [128, 4], "float32"), "bc": ("sbuf", [128, 1], "float32"), "ini": ("sbuf", [128, 1], "float32"),
     "uoi": ("sbuf", [128, 16], "int32"), "uoj": ("sbuf", [128, 16], "int32"), "uou": ("sbuf", [128, 16], "uint16"),
     "jm": ("sbuf", [128, C], "float32"), "ramp": ("sbuf", [128, C], "float32"), "jv": ("sbuf", [128, L * SLOTS], "float32"),
@@ -50,10 +53,10 @@ for _k in range(3):
     SCRATCH["bl%d" % _k] = ("sbuf", [128, 2 * L], "bfloat16")
     SCRATCH["bb%d" % _k] = ("sbuf", [128, L * SLOTS], "bfloat16")
     SCRATCH["hq%d" % _k] = ("sbuf", [128, L], "uint16")
-    SCRATCH["ca%d" % _k] = ("sbuf", [128, C // 2], F8)
+    SCRATCH["ca%d" % _k] = ("sbuf", [128, 16 * LA], F8)
     SCRATCH["sa%d" % _k] = ("sbuf", [128, C], "uint8")
 
-SEMAPHORES = ["ve", "se", "pe", "gp", "dx", "du", "dh", "dg", "dw", "dv", "ig", "do", "sent", "rz", "rh"]
+SEMAPHORES = ["ve", "se", "pe", "gp", "dx", "du", "dn", "dh", "dg", "dw", "dv", "de", "do", "sent", "rz", "rh"]
 for _k in range(3):
     SEMAPHORES += ["c%d" % _k, "ba%d" % _k, "bz%d" % _k, "h%d" % _k, "rc%d" % _k, "rb%d" % _k]
 
@@ -78,6 +81,10 @@ def handers(topo, core, partner):
     return [c for c in r if topo.die(c) == topo.die(core)], [c for c in r if topo.die(c) != topo.die(core)]
 
 
+def host_tables(near, far):
+    return [(near[0], 0, 0, L), (far[0], 1, 0, L), (near[1], 2, 0, LA), (far[1], 2, LA, L)]
+
+
 def u8(v):
     return v.bitcast(dt.uint8)
 
@@ -86,18 +93,17 @@ def hand_on(g, core, T, topo, home, near, far):
     rank = T.rank_of(home)
     mates = [T.cores[rank ^ s] for s in STEP]
     sent = 0
+    for i, (c, k, a, e) in enumerate(host_tables(near, far)):
+        if c == core:
+            g.wait_ge(T.sem.rh, len(share(topo, home, core, i, 4)))
+            sent += send(g, core, T, topo, [(mates[k], T.hr[:, a:e], T["hq%d" % k][:, a:e], "h%d" % k)], 1)
     if core in (near[0], far[0]):
-        i = 0 if core == near[0] else 1
-        h = C // 2
+        a, e = PARTS[0 if core == near[0] else 1]
         for k in range(3):
-            land = T["ca%d" % k]
-            g.wait_ge(T.sem["rc%d" % k], len(share(topo, home, core, i, 2)))
-            sent += send(g, core, T, topo, [(mates[k], u8(land[:, :]), u8(T["rc%d" % k][:, i * h:(i + 1) * h]), "c%d" % k)], 1)
+            g.wait_ge(T.sem["rc%d" % k], len(share(topo, home, core, 0, 1)))
+            sent += send(g, core, T, topo, [(mates[k], u8(T["ca%d" % k][:, 0:e - a]), u8(T["rc%d" % k][:, a:e]), "c%d" % k)], 1)
     else:
         i = 0 if core == near[1] else 1
-        if i:
-            g.wait_ge(T.sem.rh, len(share(topo, home, core, 0, 1)))
-            sent += send(g, core, T, topo, [(mates[k], T.hr[:, :], T["hq%d" % k][:, :], "h%d" % k) for k in range(3)], 4)
         g.wait_ge(T.sem.rz, len(share(topo, home, core, i, 2)))
         for k in range(3):
             if not i:
@@ -162,10 +168,13 @@ def rank_program(g, core, T, topo):
     def ms(ap, c, *deps):
         return op("ve", lambda: v.memset(ap, c), *deps)
 
-    def act(out, a, f, *deps, scale=1.0):
+    def qu(q, qs, t, *deps):
+        return op("ve", lambda: v.quantize_mx(q, qs, t), *deps)
+
+    def act(out, a, *deps, scale=1.0):
         if scale == 1.0:
-            return op("se", lambda: s.activation(out, a, f), *deps)
-        return op("se", lambda: s.activation(out, a, f, scale=scale), *deps)
+            return op("se", lambda: s.activation(out, a, AF.Copy), *deps)
+        return op("se", lambda: s.activation(out, a, AF.Copy, scale=scale), *deps)
 
     def mm(out, q, qs, x, xs, *deps):
         return op("pe", lambda: p.matmul_mx(out, q, qs, x, xs, True, True), *deps)
@@ -173,84 +182,76 @@ def rank_program(g, core, T, topo):
     def out_to(parts, n):
         sent[0] += send(g, core, T, topo, parts, n)
 
-    g.sync.dma_start(T.xt0[:, :], T.x[:, :]).then_inc(T.sem.dx, 16)
+    g.sync.dma_start(T.htj[:, :], T.ht[:, :]).then_inc(T.sem.dn, 16)
     g.sync.dma_start(T.ut[:, :], T.u[:, :]).then_inc(T.sem.du, 16)
-    nh = 0
-    g.scalar.dma_start(T.hti[:, 2 * L:3 * L], T.ht[:, :]).then_inc(T.sem.dh, 16)
+    g.sync.dma_start(T.xt0[:, :], T.x[:, :]).then_inc(T.sem.dx, 16)
     for d in range(2):
         w = 16 * (d + 1)
-        g.scalar.dma_start(T.hti[w:128, L * d:L * d + L], T.ht[0:128 - w, :]).then_inc(T.sem.dh, 16)
-        g.scalar.dma_start(T.hti[0:w, L * d:L * d + L], T.ht[128 - w:128, :]).then_inc(T.sem.dh, 16)
-    dh = ("dh", 80)
-    for d in range(SLOTS):
-        w = d + 1
-        c = slice(88 * d, 88 * d + 88)
-        if w < 8:
-            g.scalar.dma_start(T.glx[8 * w:64, c], T.gl[0:128 - 16 * w, :]).then_inc(T.sem.dg, 16)
-            nh += 16
-        g.scalar.dma_start(T.glx[0:8 * w, c], T.gl[128 - 16 * w:128, :]).then_inc(T.sem.dg, 16)
-        nh += 16
-    dg = ("dg", nh)
+        g.sync.dma_start(T.hti[w:128, L * d:L * d + L], T.ht[0:128 - w, :]).then_inc(T.sem.dh, 16)
+        g.sync.dma_start(T.hti[0:w, L * d:L * d + L], T.ht[128 - w:128, :]).then_inc(T.sem.dh, 16)
+    for i in range(16):
+        a = i % 8
+        g.scalar.dma_start(T.glc[:, 88 * i:88 * i + 88], T.gl[16 * a:16 * a + 16, :]).then_inc(T.sem.dg, 16)
+    need("sy", ("dg", 256))
+    for i in range(16):
+        a = i // 2
+        g.sync.dma_start(T.eo[8 * i:8 * i + 8, :], T.glc[:, 88 * a:88 * a + 88 * SLOTS]).then_inc(T.sem.de, 16)
 
     def iota(ap, pat, base, cm, f=False):
         if f:
             return op("gp", lambda: g.iota(ap, pat, base, cm, allow_small_or_imprecise_dtypes=True))
         return op("gp", lambda: g.iota(ap, pat, base, cm))
-    k_hlf = ms(T.hlf[:, :], 0.5)
-    k_one = ms(T.idn1[:, :], 1.0)
     k_zb = ms(T.zb[:, :], 0.0)
+    k_et = ms(T.et[:, :], 0.0)
+    k_one = ms(T.idn1[:, :], 1.0)
+    k_hlf = ms(T.hlf[:, :], 0.5)
     k_bc = ms(T.bc[:, :], -2.0 ** -110)
     g_pc = iota(T.pc[:, :], [[1, 1]], 0, 1)
     g_uo = iota(T.uoi[:, :], [[-16, 2], [16, 8]], 112, 0)
     g_jm = iota(T.jm[:, :], [[0, L], [1, 16]], 0, 0, True)
-    g_rm = iota(T.ramp[:, :], [[1, C]], 0, 0, True)
-    g_jv = iota(T.jv[:, :], [[0, SLOTS], [16, L]], 0, 0, True)
-    g_mh = op("gp", lambda: g.affine_select(T.mh[:, :], T.hlf[:, :], [[-16, SLOTS], [0, L]], A.is_ge, 0.0, -16, 1), k_hlf)
-    g_id = op("gp", lambda: g.affine_select(T.idn[:, :], T.idn1[:, :], [[-1, 128]], A.is_equal, 0.0, 0, 1), k_one)
+    need("gp", k_zb)
+    out_to([(near[1], T.zb[:, :], T.lb[0:128, :], "rz"), (far[1], T.zb[:, :], T.lb[0:128, :], "rz")], 2)
     k_p15 = ts(T.pi[:, 0:1], T.pc[:, :], 15, None, A.bitwise_and, deps=(g_pc,))
     k_h = ts(T.pi[:, 1:2], T.pc[:, :], 3, 1, A.logical_shift_right, A.bitwise_and)
-    k_i1 = ts(T.pi[:, 2:3], T.pc[:, :], 1, 120, A.logical_shift_right, A.bitwise_and)
-    k_i2 = ts(T.pi[:, 3:4], T.pc[:, :], 7, None, A.bitwise_and)
     k_uo = ts(T.uoj[:, :], T.uoi[:, :], 127, None, A.bitwise_and, deps=(g_uo,))
     k_pf = cp(T.pf[:, 0:2], T.pi[:, 0:2], k_p15, k_h)
-    k_ix = tt(T.ixt[:, :], T.pi[:, 2:3], T.pi[:, 3:4], A.add, k_i1, k_i2)
     k_uu = cp(T.uou[:, :], T.uoj[:, :], k_uo)
     k_nh = ts(T.pf[:, 2:3], T.pf[:, 1:2], -1.0, 1.0, A.mult, A.add, deps=(k_pf,))
     k_mask = ts(T.mask[:, :], T.jm[:, :], T.pf[:, 0:1], None, A.is_equal, deps=(g_jm, k_pf))
     k_keep = ts(T.keep[:, :], T.jm[:, :], T.pf[:, 0:1], None, A.not_equal)
-    k_htn = cp(T.htn[:, :], T.hti[:, 2 * L:3 * L], dh)
-    k_hto = cp(T.hto[:, :], T.hti[:, 0:2 * L])
-    k_u = op("ve", lambda: v.quantize_mx(T.uq[:, :], T.us[:, :], T.ut[:, :]), ("du", 16))
+    k_htn = cp(T.htn[:, :], T.htj[:, :], ("dn", 16))
+    m2 = cp(T.mask2[:, :], T.mask[:, :], k_mask)
+    m2 = ms(T.mask2[0:16, :], 0.0, m2)
+    k_u = qu(T.uq[:, :], T.us[:, :], T.ut[:, :], ("du", 16))
     k_up = cp(T.uqp[:, :].bitcast(dt.uint32), T.uq[:, :].bitcast(dt.uint32).indirect(T.uou[:, :]), k_u, k_uu)
-    k_us = act(T.usp[:, :], T.us[:, :].indirect(T.uou[:, :]), AF.Copy, k_u, k_uu)
+    k_us = act(T.usp[:, :], T.us[:, :].indirect(T.uou[:, :]), k_u, k_uu)
+    need("gp", k_htn)
+    out_to([(c, T.htn[:, :], T.hr[:, :], "rh") for c, _, _, _ in host_tables(near, far)], 4)
 
-    need("gp", k_htn, k_zb)
-    out_to([(far[1], T.htn[:, :], T.hr[:, :], "rh")], 1)
-    out_to([(near[1], T.zb[:, :], T.lb[0:128, :], "rz"), (far[1], T.zb[:, :], T.lb[0:128, :], "rz")], 2)
-
-    xtok, k_tab, k_eq, k_static, pdread = [("dx", 16)], None, None, None, []
-    pltok = None
-    h = C // 2
-    for k in range(3):
+    xtok, pdread, addread = [[("dx", 16)], [("dx", 16)]], [], []
+    for k in range(4):
         xt, xq, xs = T["xt%d" % k], T["xq%d" % k], T["xs%d" % k]
+        q0 = []
+        for i, (a, e) in enumerate(PARTS):
+            q0.append(qu(xq[:, a:e], xs[:, a:e], xt[:, 4 * a:4 * e], xtok[i]))
+            if k < 3:
+                need("gp", q0[i])
+                out_to([((near[0], far[0])[i], u8(xq[:, a:e]), u8(T["ca%d" % k][:, 0:e - a]), "rc%d" % k)], 1)
+        if k == 3:
+            break
         rc, rs, bl, bb, hq = T["rc%d" % k], T["rs%d" % k], T["bl%d" % k], T["bb%d" % k], T["hq%d" % k]
         zt, zq, zs, xn = T["zt%d" % k], T["zq%d" % k], T["zs%d" % k], T["xt%d" % (k + 1)]
-        mate = mates[k]
-        back = handers(topo, mate, core)
-        q0 = op("ve", lambda: v.quantize_mx(xq[:, :], xs[:, :], xt[:, :]), xtok)
-        need("gp", q0)
-        out_to([(far[0], u8(xq[:, h:C]), u8(T["ca%d" % k][:, :]), "rc%d" % k)][:0] +
-               [(near[0], u8(xq[:, 0:h]), u8(T["ca%d" % k][:, :]), "rc%d" % k), (far[0], u8(xq[:, h:C]), u8(T["ca%d" % k][:, :]), "rc%d" % k)], 2)
+        back = handers(topo, mates[k], core)
         out_to([(near[1], xs[:, :], T["sa%d" % k][:, :], "rc%d" % k)], 1)
         if k == 0:
-            need("gp", k_ix, dg)
-            g.indirect_dma_start(T.eo[:, :], None, T.glx[:], IndirectOffsetOnAxis(ap=T.ixt[:, 0:1], axis=0), bounds_check=63).then_inc(T.sem.ig, 16)
+            g_id = op("gp", lambda: g.affine_select(T.idn[:, :], T.idn1[:, :], [[-1, 128]], A.is_equal, 0.0, 0, 1), k_one)
+            k_hto = cp(T.hto[:, :], T.hti[:, :], ("dh", 64))
         sgn = []
         for d in range(2):
             m = mm(T.pd[:, 512 * d:512 * d + C], T.uqp[:, 128 * d:128 * d + 128], T.usp[:, 128 * d:128 * d + 128], xq[:, :], xs[:, :], q0, k_up, k_us, pdread)
             need("se", m, k_bc)
             sgn.append(op("se", lambda d=d: s.activation(T.sg[:, C * d:C * d + C], T.pd[:, 512 * d:512 * d + C], AF.Sign, bias=T.bc[:, 0:1])))
-        k64 = act(T.x64[:, :], xt[:, :], AF.Copy, xtok, scale=64.0)
+        k64 = act(T.x64[:, :], xt[:, :], xtok, scale=64.0)
         gs = [tt(T.gm[:, C * d:C * d + C], T.sg[:, C * d:C * d + C].indirect(T.hto[:, L * d:L * d + L]), T.mask[:, :], A.mult, sgn[d], k_hto, k_mask) for d in range(2)]
         sc = [op("ve", lambda d=d: v.tensor_tensor_scan(T.sc[:, C * d:C * d + C], T.keep[:, :], T.gm[:, C * d:C * d + C], 0.0, A.mult, A.add), gs[d], k_keep) for d in range(2)]
         k_bl = cp(bl[:, :], T.sc[:, 15:2 * C:16], sc)
@@ -261,26 +262,27 @@ def rank_program(g, core, T, topo):
         else:
             out_to([(c, bl[:, :], T.lb[a:a + 128, :], "rb%d" % k) for a in (384, 512) for c in (near[1], far[1])], 4)
         if k == 0:
-            z = ms(T.et[:, :], 0.0)
-            ec = [cp(T.et[:, 512 * b + b:512 * b + 512:4], T.idn[:, :], z, g_id) for b in range(4)]
-            k_eq = op("ve", lambda: v.quantize_mx(T.eq[:, :], T.es[:, :], T.et[:, :]), ec)
-            m2 = cp(T.mask2[:, :], T.mask[:, :])
-            m2 = ms(T.mask2[0:16, :], 0.0, m2)
+            g_jv = iota(T.jv[:, :], [[0, SLOTS], [16, L]], 0, 0, True)
+            g_mh = op("gp", lambda: g.affine_select(T.mh[:, :], T.hlf[:, :], [[-16, SLOTS], [0, L]], A.is_ge, 0.0, -16, 1), k_hlf)
+            g_rm = iota(T.ramp[:, :], [[1, C]], 0, 0, True)
+            ec = [cp(T.et[:, 512 * b + b:512 * b + 512:4], T.idn[:, :], k_et, g_id) for b in range(4)]
             a0 = ts(T.a0[:, :], T.mask[:, :], -1000.0, None, A.mult)
             a0 = ts(T.a0[0:16, :], T.jm[0:16, :], 0.0, 16.0, A.is_equal, A.mult, deps=(a0,))
             a0 = ms(T.a0[0:16, 0:1], 0.0, a0)
             i0 = ms(T.ini[:, :], 0.0)
+            k_eq = qu(T.eq[:, :], T.es[:, :], T.et[:, :], ec)
             i0 = cp(T.ini[0:16, :], T.pf[0:16, 0:1], i0)
             k_static = [m2, a0, i0]
             mh = ms(T.mh[0:16, :], 0.5, g_mh)
             jp = ts(T.jp[:, :], T.jv[:, :], T.pf[:, 0:1], None, A.add, deps=(g_jv,))
             mc = ts(T.mc[:, :], T.mh[:, :], -2.0, 1.0, A.mult, A.add, deps=(mh,))
             ji = tt(T.ji[:, :], T.jp[:, :], T.mc[:, :], A.mult, jp, mc)
-            e1 = ts(T.t1[:, :], T.eo[:, 0:88 * SLOTS:2], T.pf[:, 2:3], None, A.mult, deps=(("ig", 16), k_nh))
+            e1 = ts(T.t1[:, :], T.eo[:, 0:88 * SLOTS:2], T.pf[:, 2:3], None, A.mult, deps=(("de", 256), k_nh))
             e2 = ts(T.t2[:, :], T.eo[:, 1:88 * SLOTS:2], T.pf[:, 1:2], None, A.mult)
             e3 = tt(T.sel[:, :], T.t1[:, :], T.t2[:, :], A.add, e1, e2)
             for d in range(SLOTS):
-                ee, oo = T.sel[:, 44 * d:44 * d + L], T.sel[:, 44 * d + L:44 * d + 2 * L]
+                c = 44 * (SLOTS - 1 - d)
+                ee, oo = T.sel[:, c:c + L], T.sel[:, c + L:c + 2 * L]
                 sm = tt(T.sm[:, L * d:L * d + L], ee, oo, A.add, e3)
                 df = tt(T.df[:, L * d:L * d + L], oo, ee, A.subtract)
             em = tt(T.em[:, :], T.sm[:, :], T.mh[:, :], A.mult, sm)
@@ -296,12 +298,12 @@ def rank_program(g, core, T, topo):
         dc = []
         for b in range(4):
             m = mm(T.pd[:, 512 * b:512 * b + C], T.eq[:, 128 * b:128 * b + 128], T.es[:, 128 * b:128 * b + 128], rc[:, :], rs[:, :], call, k_eq, sgn)
-            dc.append(act(T.ds[:, C * b:C * b + C], T.pd[:, 512 * b:512 * b + C], AF.Copy, m))
+            dc.append(act(T.ds[:, C * b:C * b + C], T.pd[:, 512 * b:512 * b + C], m))
         pdread = dc
+        hs = ("h%d" % k, sum(len(share(topo, c, core, 0, 1)) for c, kk, _, _ in host_tables(*back) if kk == k))
 
         def larger(b):
-            return tt(T.mm[:, C * b:C * b + C], T.ds[:, C * b:C * b + C].indirect(hq[:, :]), xt[:, b:4 * C:4], A.max,
-                      dc[b], ("h%d" % k, len(share(topo, back[1][1], core, 0, 4))))
+            return tt(T.mm[:, C * b:C * b + C], T.ds[:, C * b:C * b + C].indirect(hq[:, :]), xt[:, b:4 * C:4], A.max, dc[b], hs)
 
         def lists(a, e, *deps):
             n1 = tt(T.nt[:, a:e], bb[:, a:e], T.dtab[:, a:e], A.mult, k_tab, *deps)
@@ -309,34 +311,56 @@ def rank_program(g, core, T, topo):
             return cp(T.nu[:, a:e], T.nf[:, a:e], n2)
         ba = ("ba%d" % k, 2 * len(share(topo, back[0][1], core, 0, 2)))
         bz = ("bz%d" % k, 2 * len(share(topo, back[1][1], core, 0, 2)))
-        lg = [larger(0), larger(1)]
+        lg = [larger(b) for b in range(3)]
         n1 = lists(0, 2 * L, ba)
         n2 = lists(2 * L, L * SLOTS, bz)
-        lg += [larger(2), larger(3)]
-        win, tok, ys = T.ramp, g_rm, [T.ya, T.yb]
+        lg += [larger(3)]
+        win, tok, ys = T.ramp, [g_rm], [T.ya, T.yb]
         for d in range(6):
-            o = ys[d % 2]
-            tok = act(o[:, :], win[:, :].indirect(T.nu[:, L * d:L * d + L]), AF.Copy, tok, n1 if d < 2 else n2)
+            o, n = ys[d % 2], n1 if d < 2 else n2
+            c = L * d
+            if d < 2:
+                tok = [act(o[:, :], win[:, :].indirect(T.nu[:, c:c + L]), tok, n)]
+            else:
+                h = 16 * LA
+                tok = [cp(o[:, 0:h], win[:, :].indirect(T.nu[:, c:c + LA]), tok, n), act(o[:, h:C], win[:, :].indirect(T.nu[:, c + LA:c + L]), tok, n)]
             win = o
         c6 = tt(T.mk2[:, :], win[:, :].indirect(T.nu[:, 6 * L:7 * L]), T.mask2[:, :], A.mult, tok, k_static)
         c7 = op("ve", lambda: v.tensor_tensor_scan(T.sc2[:, :], T.a0[:, :], T.mk2[:, :], T.ini[:, 0:1], A.add, A.max), c6)
         k_vl = cp(T.vl[:, :], T.sc2[:, 15:C:16], c7)
-        zc = []
-        for b in range(4):
-            o, w = zt[:, b:4 * C:4], T.mm[:, C * b:C * b + C].indirect(T.vl[:, :])
-            zc.append(cp(o, w, k_vl, lg) if b < 2 else act(o, w, AF.Copy, k_vl, lg))
+        zc = [[], []]
+
+        def mosaic(i, b, e):
+            a, z = PARTS[i]
+            o, w = zt[:, 4 * a + b:4 * z:4], T.mm[:, C * b:C * b + C].indirect(T.vl[:, a // 16:z // 16])
+            zc[i].append(cp(o, w, k_vl, lg) if e == "ve" else act(o, w, k_vl, lg))
+        for i, b, e in ((0, 0, "ve"), (0, 2, "se"), (0, 1, "ve"), (0, 3, "se"), (1, 0, "ve"), (1, 2, "se"), (1, 3, "se"), (1, 1, "se")):
+            mosaic(i, b, e)
         if k == 2:
             o = ys[0]
-            t6 = act(o[:, :], win[:, :].indirect(T.nu[:, 6 * L:7 * L]), AF.Copy, tok)
-            pltok = act(T.plr[:, :], o[:, :].indirect(T.nu[:, 7 * L:8 * L]), AF.Copy, t6)
-        qz = op("ve", lambda: v.quantize_mx(zq[:, :], zs[:, :], zt[:, :]), zc)
-        xtok = []
-        for b in range(4):
-            m = mm(T.pw[:, 512 * b:512 * b + C], T.wq[:, 128 * b:128 * b + 128], T.wsc[:, 128 * b:128 * b + 128], zq[:, :], zs[:, :], qz, ("dw", 32))
-            ad = tt(T.tf[:, C * b:C * b + C], T.pw[:, 512 * b:512 * b + C], T.x64[:, b:4 * C:4], A.add, m, k64)
-            xtok.append(act(xn[:, b:4 * C:4], T.tf[:, C * b:C * b + C], AF.Copy, ad, scale=2.0 ** -6))
+            t6 = act(o[:, :], win[:, :].indirect(T.nu[:, 6 * L:7 * L]), tok)
+        xtok = [[], []]
+
+        def layer(i):
+            a, z = PARTS[i]
+            qz = qu(zq[:, a:z], zs[:, a:z], zt[:, 4 * a:4 * z], zc[i])
+            ps = (T.pw, T.pd)[i]
+            return [mm(ps[:, 512 * b:512 * b + z - a], T.wq[:, 128 * b:128 * b + 128], T.wsc[:, 128 * b:128 * b + 128], zq[:, a:z], zs[:, a:z], qz, ("dw", 32), pdread, addread) for b in range(4)]
+
+        def state(i, b, m):
+            a, z = PARTS[i]
+            ps = (T.pw, T.pd)[i]
+            ad = tt(T.tf[:, C * b + a:C * b + z], ps[:, 512 * b:512 * b + z - a], T.x64[:, 4 * a + b:4 * z:4], A.add, m, k64)
+            xtok[i].append(act(xn[:, 4 * a + b:4 * z:4], T.tf[:, C * b + a:C * b + z], ad, scale=2.0 ** -6))
+            return ad
+        ma = layer(0)
+        mb = layer(1)
+        addread = [state(0, b, ma[b]) for b in range(4)] + [state(1, b, mb[b]) for b in range(4)]
+        pdread = pdread + addread
         if k == 0:
-            k_v = op("ve", lambda: v.quantize_mx(T.vq[:, :], T.vs[:, :], T.vt[:, :]), ("dv", 16))
+            k_v = qu(T.vq[:, :], T.vs[:, :], T.vt[:, :], ("dv", 16))
+        if k == 2:
+            pltok = act(T.plr[:, :], ys[0][:, :].indirect(T.nu[:, 7 * L:8 * L]), t6)
 
     do = [0]
 
@@ -344,15 +368,16 @@ def rank_program(g, core, T, topo):
         need("sy", *deps)
         g.sync.dma_start(out, a).then_inc(T.sem.do, 16)
         do[0] += 16
-    store(T.pl[0:7, :], T.plr[16:128:16, :], pltok)
-    store(T.pl[7:8, :], T.plr[0:1, :])
-    q3 = op("ve", lambda: v.quantize_mx(T.xq3[:, :], T.xs3[:, :], T.xt3[:, :]), xtok)
-    m = mm(T.pd[:, 0:C], T.vq[:, :], T.vs[:, :], T.xq3[:, :], T.xs3[:, :], q3, k_v, pdread)
-    yc = cp(T.yt[:, :], T.pd[:, 0:C], m)
-    store(T.oc[:, :], u8(T.xq3[:, :]), q3)
-    store(T.y[:, :], T.yt[:, :], yc)
+    yc = []
+    for i, (a, e) in enumerate(PARTS):
+        m = mm(T.pd[:, 512 * i:512 * i + e - a], T.vq[:, :], T.vs[:, :], T.xq3[:, a:e], T.xs3[:, a:e], q0[i], k_v, pdread)
+        yc.append(cp(T.yt[:, a:e], T.pd[:, 512 * i:512 * i + e - a], m) if i else act(T.yt[:, a:e], T.pd[:, 0:e - a], m))
+    store(T.oc[:, :], u8(T.xq3[:, :]), q0)
     for b in range(4):
         store(T.osc[4 * b:4 * b + 4, :], T.xs3[32 * b:32 * b + 4, :])
+    store(T.y[:, :], T.yt[:, :], yc)
+    store(T.pl[0:7, :], T.plr[16:128:16, :], pltok)
+    store(T.pl[7:8, :], T.plr[0:1, :])
     g.sync.wait_ge(T.sem.do, do[0])
     for e in ("ve", "se", "pe", "gp"):
         need("gp", (e, count[e]))

from concourse.bass import DstId, RemoteDMATransfer
from concourse.mybir import dt, AluOpType, ActivationFunctionType

C = 352
STEP = [1, 2, 4]
L = C // 16
LA = 12
PARTS = [(0, 16 * LA), (16 * LA, C)]
SLOTS = 8
F8 = "float8_e4m3fn_x4"

SCRATCH = {
    "ut": ("sbuf", [128, 512], "bfloat16"), "uq": ("sbuf", [128, 128], F8), "us": ("sbuf", [128, 128], "uint8"),
    "uqp": ("sbuf", [128, 256], F8), "usp": ("sbuf", [128, 256], "uint8"),
    "vt": ("sbuf", [128, 512], "bfloat16"), "vq": ("sbuf", [128, 128], F8), "vs": ("sbuf", [128, 128], "uint8"),
    "wq": ("sbuf", [128, 512], F8), "wsc": ("sbuf", [128, 512], "uint8"),
    "idn1": ("sbuf", [128, 128], "float32"), "idn": ("sbuf", [128, 128], "float32"),
    "et": ("sbuf", [128, 2048], "bfloat16"), "eq": ("sbuf", [128, 512], F8), "es": ("sbuf", [128, 512], "uint8"),
    "hti": ("sbuf", [128, 2 * L], "int32"), "htj": ("sbuf", [128, L], "int32"),
    "hto": ("sbuf", [128, 2 * L], "uint16"), "htn": ("sbuf", [128, L], "uint16"),
    "glc": ("dram", [8, 2 * 88 * SLOTS], "int32"), "eo": ("sbuf", [128, 88 * SLOTS], "int32"),
    "pc": ("sbuf", [128, 1], "int32"), "pi": ("sbuf", [128, 8], "int32"),
    "pf": ("sbuf", [128, 4], "float32"), "bc": ("sbuf", [128, 1], "float32"), "ini": ("sbuf", [128, 1], "float32"),
    "uoi": ("sbuf", [128, 16], "int32"), "uoj": ("sbuf", [128, 16], "int32"), "uou": ("sbuf", [128, 16], "uint16"),
    "jm": ("sbuf", [128, C], "float32"), "ramp": ("sbuf", [128, C], "float32"), "jv": ("sbuf", [128, L * SLOTS], "float32"),
    "jp": ("sbuf", [128, L * SLOTS], "float32"), "hlf": ("sbuf", [128, L * SLOTS], "float32"), "mh": ("sbuf", [128, L * SLOTS], "float32"),
    "mc": ("sbuf", [128, L * SLOTS], "float32"), "ji": ("sbuf", [128, L * SLOTS], "float32"),
    "mask": ("sbuf", [128, C], "bfloat16"), "keep": ("sbuf", [128, C], "bfloat16"),
    "mask2": ("sbuf", [128, C], "float32"), "a0": ("sbuf", [128, C], "float32"),
    "t1": ("sbuf", [128, 44 * SLOTS], "float32"), "t2": ("sbuf", [128, 44 * SLOTS], "float32"), "sel": ("sbuf", [128, 44 * SLOTS], "float32"),
    "sm": ("sbuf", [128, L * SLOTS], "float32"), "df": ("sbuf", [128, L * SLOTS], "float32"),
    "em": ("sbuf", [128, L * SLOTS], "float32"), "etab": ("sbuf", [128, L * SLOTS], "float32"), "dtab": ("sbuf", [128, L * SLOTS], "float32"),
    "zb": ("sbuf", [128, 2 * L], "bfloat16"),
    "sg": ("sbuf", [128, 2 * C], "bfloat16"), "gm": ("sbuf", [128, 2 * C], "bfloat16"), "sc": ("sbuf", [128, 2 * C], "bfloat16"),
    "nt": ("sbuf", [128, L * SLOTS], "float32"), "nf": ("sbuf", [128, L * SLOTS], "float32"), "nu": ("sbuf", [128, L * SLOTS], "uint16"),
    "ya": ("sbuf", [128, C], "float32"), "yb": ("sbuf", [128, C], "float32"), "plr": ("sbuf", [128, C], "float32"),
    "mk2": ("sbuf", [128, C], "float32"), "sc2": ("sbuf", [128, C], "float32"), "vl": ("sbuf", [128, L], "uint16"),
    "x64": ("sbuf", [128, 4 * C], "bfloat16"), "ds": ("sbuf", [128, 4 * C], "bfloat16"), "mm": ("sbuf", [128, 4 * C], "bfloat16"),
    "tf": ("sbuf", [128, 4 * C], "float32"), "yt": ("sbuf", [128, C], "float32"),
    "pd": ("psum", [128, 2048], "float32"), "pw": ("psum", [128, 2048], "float32"),
    "hr": ("sbuf", [128, L], "uint16"), "lb": ("dram", [640, 2 * L], "bfloat16"),
}
for _k in range(4):
    SCRATCH["xt%d" % _k] = ("sbuf", [128, 4 * C], "bfloat16")
    SCRATCH["xq%d" % _k] = ("sbuf", [128, C], F8)
    SCRATCH["xs%d" % _k] = ("sbuf", [128, C], "uint8")
for _k in range(3):
    SCRATCH["rc%d" % _k] = ("sbuf", [128, C], F8)
    SCRATCH["rs%d" % _k] = ("sbuf", [128, C], "uint8")
    SCRATCH["zt%d" % _k] = ("sbuf", [128, 4 * C], "bfloat16")
    SCRATCH["zq%d" % _k] = ("sbuf", [128, C], F8)
    SCRATCH["zs%d" % _k] = ("sbuf", [128, C], "uint8")
    SCRATCH["bl%d" % _k] = ("sbuf", [128, 2 * L], "bfloat16")
    SCRATCH["bb%d" % _k] = ("sbuf", [128, L * SLOTS], "bfloat16")
    SCRATCH["hq%d" % _k] = ("sbuf", [128, L], "uint16")
    SCRATCH["ca%d" % _k] = ("sbuf", [128, 16 * LA], F8)
    SCRATCH["sa%d" % _k] = ("sbuf", [128, C], "uint8")

SEMAPHORES = ["ve", "se", "pe", "gp", "dx", "du", "dn", "dh", "dg", "dw", "dv", "de", "do", "sent", "rz", "rh"]
for _k in range(3):
    SEMAPHORES += ["c%d" % _k, "ba%d" % _k, "bz%d" % _k, "h%d" % _k, "rc%d" % _k, "rb%d" % _k]


def share(topo, src, dst, i, n):
    return topo.engines(src, dst)[i::n]


def send(g, core, T, topo, parts, n):
    ts, total = [], 0
    for i, (dst, a, b, sem) in enumerate(parts):
        e = share(topo, core, dst, i, n)
        rid, pid = topo.addr(dst, core)
        ts.append(RemoteDMATransfer(dst_ids=[DstId(rid=rid, pnc=pid)], dma_engine_mask=sum(1 << j for j in e), remote_sem=T.sem[sem], srcs=[a], dsts=[b]))
        total += len(e)
    g.remote_dma_fused(ts, local_sem=T.sem.sent)
    return total


def handers(topo, core, partner):
    r = [c for c in topo.cores_of(core) if c != core and topo.may_write(c, partner)]
    return [c for c in r if topo.die(c) == topo.die(core)], [c for c in r if topo.die(c) != topo.die(core)]


def host_tables(near, far):
    return [(near[0], 0, 0, L), (far[0], 1, 0, L), (near[1], 2, 0, LA), (far[1], 2, LA, L)]


def u8(v):
    return v.bitcast(dt.uint8)


def hand_on(g, core, T, topo, home, near, far):
    rank = T.rank_of(home)
    mates = [T.cores[rank ^ s] for s in STEP]
    sent = 0
    for i, (c, k, a, e) in enumerate(host_tables(near, far)):
        if c == core:
            g.wait_ge(T.sem.rh, len(share(topo, home, core, i, 4)))
            sent += send(g, core, T, topo, [(mates[k], T.hr[:, a:e], T["hq%d" % k][:, a:e], "h%d" % k)], 1)
    if core in (near[0], far[0]):
        a, e = PARTS[0 if core == near[0] else 1]
        for k in range(3):
            g.wait_ge(T.sem["rc%d" % k], len(share(topo, home, core, 0, 1)))
            sent += send(g, core, T, topo, [(mates[k], u8(T["ca%d" % k][:, 0:e - a]), u8(T["rc%d" % k][:, a:e]), "c%d" % k)], 1)
    else:
        i = 0 if core == near[1] else 1
        g.wait_ge(T.sem.rz, len(share(topo, home, core, i, 2)))
        for k in range(3):
            if not i:
                g.wait_ge(T.sem["rc%d" % k], len(share(topo, home, core, 0, 1)))
                sent += send(g, core, T, topo, [(mates[k], T["sa%d" % k][:, :], T["rs%d" % k][:, :], "c%d" % k)], 1)
            if k < 2:
                g.wait_ge(T.sem["rb%d" % k], len(share(topo, home, core, i, 2)))
                base = 128 * (k + 1)
            else:
                g.wait_ge(T.sem["rb%d" % k], 2 * len(share(topo, home, core, 0, 4)))
                base = 512
            parts = []
            for m in (2 * i, 2 * i + 1):
                a = base - 32 * m
                parts.append((mates[k], T.lb[a:a + 128, :], T["bb%d" % k][:, 2 * L * m:2 * L * (m + 1)], ("bz%d" if i else "ba%d") % k))
            sent += send(g, core, T, topo, parts, 2)
    g.wait_ge(T.sem.sent, sent)


def rank_program(g, core, T, topo):
    rank = T.rank_of(core)
    if rank is None:
        for home in T.cores:
            if core in topo.cores_of(home):
                near, far = handers(topo, home, T.cores[T.rank_of(home) ^ STEP[0]])
                if core in near[:2] + far[:2]:
                    hand_on(g, core, T, topo, home, near, far)
        return
    A, AF = AluOpType, ActivationFunctionType
    mates = [T.cores[rank ^ s] for s in STEP]
    near, far = handers(topo, core, mates[0])
    queue = {"ve": g.vector, "se": g.scalar, "pe": g.tensor, "gp": g, "sy": g.sync}
    count, seen, sent = {"ve": 0, "se": 0, "pe": 0, "gp": 0}, {}, [0]

    def need(e, *toks):
        for t in toks:
            if isinstance(t, list):
                need(e, *t)
            elif t is not None and seen.get((e, t[0]), 0) < t[1]:
                queue[e].wait_ge(T.sem[t[0]], t[1])
                seen[(e, t[0])] = t[1]

    def op(e, call, *deps):
        need(e, *deps)
        count[e] += 1
        call().then_inc(T.sem[e], 1)
        return (e, count[e])

    v, s, p = g.vector, g.scalar, g.tensor

    def ts(out, in0, s1, s2, o0, o1=None, deps=()):
        if o1 is None:
            return op("ve", lambda: v.tensor_scalar(out, in0, s1, None, o0), *deps)
        return op("ve", lambda: v.tensor_scalar(out, in0, s1, s2, o0, o1), *deps)

    def tt(out, a, b, o, *deps):
        return op("ve", lambda: v.tensor_tensor(out, a, b, o), *deps)

    def cp(out, a, *deps):
        return op("ve", lambda: v.tensor_copy(out, a), *deps)

    def ms(ap, c, *deps):
        return op("ve", lambda: v.memset(ap, c), *deps)

    def qu(q, qs, t, *deps):
        return op("ve", lambda: v.quantize_mx(q, qs, t), *deps)

    def act(out, a, *deps, scale=1.0):
        if scale == 1.0:
            return op("se", lambda: s.activation(out, a, AF.Copy), *deps)
        return op("se", lambda: s.activation(out, a, AF.Copy, scale=scale), *deps)

    def mm(out, q, qs, x, xs, *deps):
        return op("pe", lambda: p.matmul_mx(out, q, qs, x, xs, True, True), *deps)

    def out_to(parts, n):
        sent[0] += send(g, core, T, topo, parts, n)

    g.sync.dma_start(T.htj[:, :], T.ht[:, :]).then_inc(T.sem.dn, 16)
    g.sync.dma_start(T.ut[:, :], T.u[:, :]).then_inc(T.sem.du, 16)
    g.sync.dma_start(T.xt0[:, :], T.x[:, :]).then_inc(T.sem.dx, 16)
    for d in range(2):
        w = 16 * (d + 1)
        g.sync.dma_start(T.hti[w:128, L * d:L * d + L], T.ht[0:128 - w, :]).then_inc(T.sem.dh, 16)
        g.sync.dma_start(T.hti[0:w, L * d:L * d + L], T.ht[128 - w:128, :]).then_inc(T.sem.dh, 16)
    for i in range(16):
        a = i % 8
        g.scalar.dma_start(T.glc[:, 88 * i:88 * i + 88], T.gl[16 * a:16 * a + 16, :]).then_inc(T.sem.dg, 16)
    need("sy", ("dg", 256))
    for i in range(16):
        a = i // 2
        g.sync.dma_start(T.eo[8 * i:8 * i + 8, :], T.glc[:, 88 * a:88 * a + 88 * SLOTS]).then_inc(T.sem.de, 16)

    def iota(ap, pat, base, cm, f=False):
        if f:
            return op("gp", lambda: g.iota(ap, pat, base, cm, allow_small_or_imprecise_dtypes=True))
        return op("gp", lambda: g.iota(ap, pat, base, cm))
    k_zb = ms(T.zb[:, :], 0.0)
    k_et = ms(T.et[:, :], 0.0)
    k_one = ms(T.idn1[:, :], 1.0)
    k_hlf = ms(T.hlf[:, :], 0.5)
    k_bc = ms(T.bc[:, :], -2.0 ** -110)
    g_pc = iota(T.pc[:, :], [[1, 1]], 0, 1)
    g_uo = iota(T.uoi[:, :], [[-16, 2], [16, 8]], 112, 0)
    g_jm = iota(T.jm[:, :], [[0, L], [1, 16]], 0, 0, True)
    need("gp", k_zb)
    out_to([(near[1], T.zb[:, :], T.lb[0:128, :], "rz"), (far[1], T.zb[:, :], T.lb[0:128, :], "rz")], 2)
    k_p15 = ts(T.pi[:, 0:1], T.pc[:, :], 15, None, A.bitwise_and, deps=(g_pc,))
    k_h = ts(T.pi[:, 1:2], T.pc[:, :], 3, 1, A.logical_shift_right, A.bitwise_and)
    k_uo = ts(T.uoj[:, :], T.uoi[:, :], 127, None, A.bitwise_and, deps=(g_uo,))
    k_pf = cp(T.pf[:, 0:2], T.pi[:, 0:2], k_p15, k_h)
    k_uu = cp(T.uou[:, :], T.uoj[:, :], k_uo)
    k_nh = ts(T.pf[:, 2:3], T.pf[:, 1:2], -1.0, 1.0, A.mult, A.add, deps=(k_pf,))
    k_mask = ts(T.mask[:, :], T.jm[:, :], T.pf[:, 0:1], None, A.is_equal, deps=(g_jm, k_pf))
    k_keep = ts(T.keep[:, :], T.jm[:, :], T.pf[:, 0:1], None, A.not_equal)
    k_htn = cp(T.htn[:, :], T.htj[:, :], ("dn", 16))
    m2 = cp(T.mask2[:, :], T.mask[:, :], k_mask)
    m2 = ms(T.mask2[0:16, :], 0.0, m2)
    k_u = qu(T.uq[:, :], T.us[:, :], T.ut[:, :], ("du", 16))
    k_up = cp(T.uqp[:, :].bitcast(dt.uint32), T.uq[:, :].bitcast(dt.uint32).indirect(T.uou[:, :]), k_u, k_uu)
    k_us = act(T.usp[:, :], T.us[:, :].indirect(T.uou[:, :]), k_u, k_uu)
    need("gp", k_htn)
    out_to([(c, T.htn[:, :], T.hr[:, :], "rh") for c, _, _, _ in host_tables(near, far)], 4)

    xtok, pdread, addread = [[("dx", 16)], [("dx", 16)]], [], []
    for k in range(4):
        xt, xq, xs = T["xt%d" % k], T["xq%d" % k], T["xs%d" % k]
        q0 = []
        for i, (a, e) in enumerate(PARTS):
            q0.append(qu(xq[:, a:e], xs[:, a:e], xt[:, 4 * a:4 * e], xtok[i]))
            if k < 3:
                need("gp", q0[i])
                out_to([((near[0], far[0])[i], u8(xq[:, a:e]), u8(T["ca%d" % k][:, 0:e - a]), "rc%d" % k)], 1)
        if k == 3:
            break
        rc, rs, bl, bb, hq = T["rc%d" % k], T["rs%d" % k], T["bl%d" % k], T["bb%d" % k], T["hq%d" % k]
        zt, zq, zs, xn = T["zt%d" % k], T["zq%d" % k], T["zs%d" % k], T["xt%d" % (k + 1)]
        back = handers(topo, mates[k], core)
        out_to([(near[1], xs[:, :], T["sa%d" % k][:, :], "rc%d" % k)], 1)
        if k == 0:
            g_id = op("gp", lambda: g.affine_select(T.idn[:, :], T.idn1[:, :], [[-1, 128]], A.is_equal, 0.0, 0, 1), k_one)
            k_hto = cp(T.hto[:, :], T.hti[:, :], ("dh", 64))
        sgn = []
        for d in range(2):
            m = mm(T.pd[:, 512 * d:512 * d + C], T.uqp[:, 128 * d:128 * d + 128], T.usp[:, 128 * d:128 * d + 128], xq[:, :], xs[:, :], q0, k_up, k_us, pdread)
            need("se", m, k_bc)
            sgn.append(op("se", lambda d=d: s.activation(T.sg[:, C * d:C * d + C], T.pd[:, 512 * d:512 * d + C], AF.Sign, bias=T.bc[:, 0:1])))
        k64 = act(T.x64[:, :], xt[:, :], xtok, scale=64.0)
        gs = [tt(T.gm[:, C * d:C * d + C], T.sg[:, C * d:C * d + C].indirect(T.hto[:, L * d:L * d + L]), T.mask[:, :], A.mult, sgn[d], k_hto, k_mask) for d in range(2)]
        sc = [op("ve", lambda d=d: v.tensor_tensor_scan(T.sc[:, C * d:C * d + C], T.keep[:, :], T.gm[:, C * d:C * d + C], 0.0, A.mult, A.add), gs[d], k_keep) for d in range(2)]
        k_bl = cp(bl[:, :], T.sc[:, 15:2 * C:16], sc)
        need("gp", k_bl)
        if k < 2:
            a = 128 * (k + 1)
            out_to([(c, bl[:, :], T.lb[a:a + 128, :], "rb%d" % k) for c in (near[1], far[1])], 2)
        else:
            out_to([(c, bl[:, :], T.lb[a:a + 128, :], "rb%d" % k) for a in (384, 512) for c in (near[1], far[1])], 4)
        if k == 0:
            g_jv = iota(T.jv[:, :], [[0, SLOTS], [16, L]], 0, 0, True)
            g_mh = op("gp", lambda: g.affine_select(T.mh[:, :], T.hlf[:, :], [[-16, SLOTS], [0, L]], A.is_ge, 0.0, -16, 1), k_hlf)
            g_rm = iota(T.ramp[:, :], [[1, C]], 0, 0, True)
            ec = [cp(T.et[:, 512 * b + b:512 * b + 512:4], T.idn[:, :], k_et, g_id) for b in range(4)]
            a0 = ts(T.a0[:, :], T.mask[:, :], -1000.0, None, A.mult)
            a0 = ts(T.a0[0:16, :], T.jm[0:16, :], 0.0, 16.0, A.is_equal, A.mult, deps=(a0,))
            a0 = ms(T.a0[0:16, 0:1], 0.0, a0)
            i0 = ms(T.ini[:, :], 0.0)
            k_eq = qu(T.eq[:, :], T.es[:, :], T.et[:, :], ec)
            i0 = cp(T.ini[0:16, :], T.pf[0:16, 0:1], i0)
            k_static = [m2, a0, i0]
            mh = ms(T.mh[0:16, :], 0.5, g_mh)
            jp = ts(T.jp[:, :], T.jv[:, :], T.pf[:, 0:1], None, A.add, deps=(g_jv,))
            mc = ts(T.mc[:, :], T.mh[:, :], -2.0, 1.0, A.mult, A.add, deps=(mh,))
            ji = tt(T.ji[:, :], T.jp[:, :], T.mc[:, :], A.mult, jp, mc)
            e1 = ts(T.t1[:, :], T.eo[:, 0:88 * SLOTS:2], T.pf[:, 2:3], None, A.mult, deps=(("de", 256), k_nh))
            e2 = ts(T.t2[:, :], T.eo[:, 1:88 * SLOTS:2], T.pf[:, 1:2], None, A.mult)
            e3 = tt(T.sel[:, :], T.t1[:, :], T.t2[:, :], A.add, e1, e2)
            for d in range(SLOTS):
                c = 44 * (SLOTS - 1 - d)
                ee, oo = T.sel[:, c:c + L], T.sel[:, c + L:c + 2 * L]
                sm = tt(T.sm[:, L * d:L * d + L], ee, oo, A.add, e3)
                df = tt(T.df[:, L * d:L * d + L], oo, ee, A.subtract)
            em = tt(T.em[:, :], T.sm[:, :], T.mh[:, :], A.mult, sm)
            dtb = tt(T.dtab[:, :], T.df[:, :], T.mh[:, :], A.mult, df)
            etb = tt(T.etab[:, :], T.em[:, :], T.ji[:, :], A.add, em, ji)
            k_tab = [dtb, etb]
        call = ("c%d" % k, sum(len(share(topo, c, core, 0, 1)) for c in (back[0][0], back[1][0], back[0][1])))
        if k == 0:
            need("sy", call)
            g.sync.dma_start(u8(T.wq[:, :]), T.wc[:, :]).then_inc(T.sem.dw, 16)
            g.sync.dma_start(T.wsc[:, :], T.ws[:, :]).then_inc(T.sem.dw, 16)
            g.sync.dma_start(T.vt[:, :], T.v[:, :]).then_inc(T.sem.dv, 16)
        dc = []
        for b in range(4):
            m = mm(T.pd[:, 512 * b:512 * b + C], T.eq[:, 128 * b:128 * b + 128], T.es[:, 128 * b:128 * b + 128], rc[:, :], rs[:, :], call, k_eq, sgn)
            dc.append(act(T.ds[:, C * b:C * b + C], T.pd[:, 512 * b:512 * b + C], m))
        pdread = dc
        hs = ("h%d" % k, sum(len(share(topo, c, core, 0, 1)) for c, kk, _, _ in host_tables(*back) if kk == k))

        def larger(b):
            return tt(T.mm[:, C * b:C * b + C], T.ds[:, C * b:C * b + C].indirect(hq[:, :]), xt[:, b:4 * C:4], A.max, dc[b], hs)

        def lists(a, e, *deps):
            n1 = tt(T.nt[:, a:e], bb[:, a:e], T.dtab[:, a:e], A.mult, k_tab, *deps)
            n2 = tt(T.nf[:, a:e], T.nt[:, a:e], T.etab[:, a:e], A.add, n1)
            return cp(T.nu[:, a:e], T.nf[:, a:e], n2)
        ba = ("ba%d" % k, 2 * len(share(topo, back[0][1], core, 0, 2)))
        bz = ("bz%d" % k, 2 * len(share(topo, back[1][1], core, 0, 2)))
        lg = [larger(b) for b in range(3)]
        n1 = lists(0, 2 * L, ba)
        n2 = lists(2 * L, L * SLOTS, bz)
        lg += [larger(3)]
        win, tok, ys = T.ramp, [g_rm], [T.ya, T.yb]
        for d in range(6):
            o, n = ys[d % 2], n1 if d < 2 else n2
            c = L * d
            if d < 2:
                tok = [act(o[:, :], win[:, :].indirect(T.nu[:, c:c + L]), tok, n)]
            else:
                h = 16 * LA
                tok = [cp(o[:, 0:h], win[:, :].indirect(T.nu[:, c:c + LA]), tok, n), act(o[:, h:C], win[:, :].indirect(T.nu[:, c + LA:c + L]), tok, n)]
            win = o
        c6 = tt(T.mk2[:, :], win[:, :].indirect(T.nu[:, 6 * L:7 * L]), T.mask2[:, :], A.mult, tok, k_static)
        c7 = op("ve", lambda: v.tensor_tensor_scan(T.sc2[:, :], T.a0[:, :], T.mk2[:, :], T.ini[:, 0:1], A.add, A.max), c6)
        k_vl = cp(T.vl[:, :], T.sc2[:, 15:C:16], c7)
        zc = [[], []]

        def mosaic(i, b, e):
            a, z = PARTS[i]
            o, w = zt[:, 4 * a + b:4 * z:4], T.mm[:, C * b:C * b + C].indirect(T.vl[:, a // 16:z // 16])
            zc[i].append(cp(o, w, k_vl, lg) if e == "ve" else act(o, w, k_vl, lg))
        for i, b, e in ((0, 0, "ve"), (0, 2, "se"), (0, 1, "ve"), (0, 3, "se"), (1, 0, "ve"), (1, 2, "se"), (1, 3, "se"), (1, 1, "se")):
            mosaic(i, b, e)
        if k == 2:
            o = ys[0]
            t6 = act(o[:, :], win[:, :].indirect(T.nu[:, 6 * L:7 * L]), tok)
        xtok = [[], []]

        def layer(i):
            a, z = PARTS[i]
            qz = qu(zq[:, a:z], zs[:, a:z], zt[:, 4 * a:4 * z], zc[i])
            ps = (T.pw, T.pd)[i]
            return [mm(ps[:, 512 * b:512 * b + z - a], T.wq[:, 128 * b:128 * b + 128], T.wsc[:, 128 * b:128 * b + 128], zq[:, a:z], zs[:, a:z], qz, ("dw", 32), pdread, addread) for b in range(4)]

        def state(i, b, m):
            a, z = PARTS[i]
            ps = (T.pw, T.pd)[i]
            ad = tt(T.tf[:, C * b + a:C * b + z], ps[:, 512 * b:512 * b + z - a], T.x64[:, 4 * a + b:4 * z:4], A.add, m, k64)
            xtok[i].append(act(xn[:, 4 * a + b:4 * z:4], T.tf[:, C * b + a:C * b + z], ad, scale=2.0 ** -6))
            return ad
        ma = layer(0)
        mb = layer(1)
        addread = [state(0, b, ma[b]) for b in range(4)] + [state(1, b, mb[b]) for b in range(4)]
        pdread = pdread + addread
        if k == 0:
            k_v = qu(T.vq[:, :], T.vs[:, :], T.vt[:, :], ("dv", 16))
        if k == 2:
            pltok = act(T.plr[:, :], ys[0][:, :].indirect(T.nu[:, 7 * L:8 * L]), t6)

    do = [0]

    def store(out, a, *deps):
        need("sy", *deps)
        g.sync.dma_start(out, a).then_inc(T.sem.do, 16)
        do[0] += 16
    yc = []
    for i, (a, e) in enumerate(PARTS):
        m = mm(T.pd[:, 512 * i:512 * i + e - a], T.vq[:, :], T.vs[:, :], T.xq3[:, a:e], T.xs3[:, a:e], q0[i], k_v, pdread)
        yc.append(cp(T.yt[:, a:e], T.pd[:, 512 * i:512 * i + e - a], m) if i else act(T.yt[:, a:e], T.pd[:, 0:e - a], m))
    store(T.oc[:, :], u8(T.xq3[:, :]), q0)
    for b in range(4):
        store(T.osc[4 * b:4 * b + 4, :], T.xs3[32 * b:32 * b + 4, :])
    store(T.y[:, :], T.yt[:, :], yc)
    store(T.pl[0:7, :], T.plr[16:128:16, :], pltok)
    store(T.pl[7:8, :], T.plr[0:1, :])
    g.sync.wait_ge(T.sem.do, do[0])
    for e in ("ve", "se", "pe", "gp"):
        need("gp", (e, count[e]))
    g.wait_ge(T.sem.sent, sent[0])
